import numpy as np
import ml_dtypes


def mxq(x, axis, fmt="e4m3"):
    dtype, down = {"e4m3": (ml_dtypes.float8_e4m3fn, 7), "e5m2": (ml_dtypes.float8_e5m2, 14)}[fmt]
    v = np.moveaxis(np.asarray(x, np.float32).astype(ml_dtypes.bfloat16).astype(np.float64), axis, -1)
    blocks = v.reshape(v.shape[:-1] + (-1, 32))
    amax = np.abs(blocks).max(-1, keepdims=True)
    byte = np.maximum(np.where(amax > 0, np.frexp(amax)[1] - 1 + 127, 0) - down, 1)
    scale = np.exp2(byte - 127.0)
    codes = (blocks / scale).astype(np.float32).astype(dtype).astype(np.float64)
    return np.moveaxis((codes * scale).reshape(v.shape), -1, axis)


WIDE = False


def mx_kscale(k):
    if not WIDE:
        return np.ones(k)
    levels = np.array([10, -10, 5, -5, 0])
    if k % 512:
        return np.exp2(np.random.permutation(np.resize(levels, k // 32))).repeat(32)
    a = np.empty((k // 512, 16))
    for p in range(k // 512):
        a[p, :8] = np.random.permutation(np.resize(levels, 8))
        for g in range(8):
            far = levels[np.abs(levels - a[p, g]) >= 10]
            a[p, g + 8] = far[np.random.randint(len(far))]
    return np.exp2(a.ravel()).repeat(32)


BF16 = ml_dtypes.bfloat16


def bf(x):
    return np.asarray(x, np.float32).astype(BF16)


def f64(x):
    return np.asarray(x).astype(np.float64)

def planes(Y):
    n, m = Y.shape
    b = f64(bf(Y)).reshape(n // 32, 32, m)
    amax = np.abs(b).max(1)
    byte = np.clip(np.where(amax > 0, np.frexp(amax)[1] - 1 + 127 - 7, 1), 1, 254)
    codes = (b * np.exp2(127.0 - byte)[:, None, :]).reshape(n, m).astype(np.float32).astype(ml_dtypes.float8_e4m3fn).view(np.uint8)
    words = codes.reshape(n // 512, 128, 4, m).transpose(0, 1, 3, 2)
    return np.ascontiguousarray(words), np.ascontiguousarray(byte.astype(np.uint8).reshape(n // 512, 16, m))


ITEMS, FEATS, USERS, HIDDEN, LATENT = 2048, 1024, 1024, 1024, 512


def setup_inputs():
    rn = np.random.randn
    sf = mx_kscale(FEATS)
    su = mx_kscale(USERS)
    t = mx_kscale(ITEMS)
    spread = np.exp(0.8 * rn(HIDDEN))
    x = rn(ITEMS, FEATS) * sf[None, :]
    enc = rn(FEATS, HIDDEN) / np.sqrt(FEATS) / sf[:, None]
    gain = ITEMS ** -0.25 * np.exp(0.3 * rn(ITEMS)) * t
    d = rn(ITEMS, USERS) / np.sqrt(USERS) * ITEMS ** -0.25 * su[None, :] / t[:, None]
    u = rn(USERS, LATENT) / su[:, None]
    proj = 0.6 * rn(HIDDEN, LATENT) * spread[:, None]
    step = 0.7 * spread
    return {"item_feats": bf(x), "encoder": bf(enc), "item_gain": bf(gain), "score_grads": bf(d),
            "user_factors": bf(u), "projection": bf(proj), "step_sizes": bf(step)}

def reference(item_feats, encoder, item_gain, score_grads, user_factors, projection, step_sizes):
    A = mxq(f64(item_feats), 1, "e4m3") @ mxq(f64(encoder), 0, "e4m3")
    Z = np.maximum(A, 0.0) * f64(item_gain)[:, None]
    G = mxq(f64(score_grads), 1, "e4m3") @ mxq(f64(user_factors), 0, "e4m3")
    grad = mxq(Z, 0, "e4m3").T @ mxq(G, 0, "e4m3")
    y = f64(projection) - f64(step_sizes)[:, None] * grad
    Y = y.reshape(HIDDEN, LATENT)
    words, scales = planes(Y)
    return y, words, scales

@@ -1,0 +1,307 @@
+from contextlib import ExitStack
+
+import concourse.mybir as mybir
+from concourse.masks import make_identity
+
+ITEMS, FEATS, USERS, HIDDEN, LATENT = 2048, 1024, 1024, 1024, 512
+FLOPS = 2 * ITEMS * (FEATS * HIDDEN + USERS * LATENT + HIDDEN * LATENT)
+
+F32 = mybir.dt.float32
+BF16 = mybir.dt.bfloat16
+I32 = mybir.dt.int32
+U32 = mybir.dt.uint32
+U8 = mybir.dt.uint8
+FP8X4 = mybir.dt.float8_e4m3fn_x4
+ALU = mybir.AluOpType
+
+P = 128
+PACK = 4
+K_PASS = P * PACK
+GROUPS = ITEMS // K_PASS
+STAGE_BUFS = 7
+TAIL_WIDTHS = ((256, 256), (256, 256))
+E_ON_SCALAR = ((0, 0), (1, 1))
+SLOT_LOADS = 2
+TAIL_TAGS = ("turn", "prod", "turn", "prod", "turn")
+ORDER = "D0 D1 G0 i00 X0 i01 q00 q01 G1 D2 A00 i10 X1 G2 q10 D3 A10 i11 X2 G3 q11 A20 X3 A01 n L30 A11 P0 A21 P1 L31 P2 P3"
+
+
+def tile_latent_projection_step_h3_kernel(
+    tc, item_feats, encoder, item_gain, score_grads, user_factors, projection, step_sizes, out_0, out_1, out_2
+):
+    nc = tc.nc
+    with ExitStack() as ctx:
+        keep = ctx.enter_context(tc.tile_pool(name="keep", bufs=1))
+        psum = ctx.enter_context(tc.psum_pool(name="psum", bufs=4))
+        ctx.enter_context(tc.manual_schedule())
+
+        def stage_tile():
+            return keep.tile([P, K_PASS * PACK], BF16, name="stage", tag="stage", bufs=STAGE_BUFS, align_bytes=64)
+
+        def mx_tiles(name, bufs=1):
+            codes = keep.tile([P, K_PASS], U32, name=name + "_codes", tag=name + "_codes", bufs=bufs, align_bytes=64)
+            scales = keep.tile([P, K_PASS], U8, name=name + "_scales", tag=name + "_scales", bufs=bufs, align_bytes=64)
+            return codes, scales
+
+        def quantize(mx, staged, cols=slice(0, K_PASS), src=None):
+            codes, scales = mx
+            src = src or slice(PACK * cols.start, PACK * cols.stop)
+            nc.vector.quantize_mx(out=codes[:, cols].bitcast(FP8X4), scales=scales[:, cols], in_=staged[:, src])
+
+        def matmul(out, lhs, lhs_cols, rhs, rhs_cols, start, stop):
+            nc.tensor.matmul_mx(
+                out=out,
+                lhsT=lhs[0][:, lhs_cols].bitcast(FP8X4),
+                lhsT_scale=lhs[1][:, lhs_cols],
+                rhs=rhs[0][:, rhs_cols].bitcast(FP8X4),
+                rhs_scale=rhs[1][:, rhs_cols],
+                start=start,
+                stop=stop,
+            )
+
+        def block(i, width=P):
+            return slice(i * width, (i + 1) * width)
+
+        ident = keep.tile([P, P], F32, name="ident")
+        make_identity(nc, ident[:])
+
+        def load_k_first(name, src):
+            raw = keep.tile([P, PACK, K_PASS], BF16, name=name)
+            nc.sync.dma_start(out=raw[:], in_=src.rearrange("(p j) n -> p j n", j=PACK))
+            return raw
+
+        def load_items(name, src, g, by_slot=False):
+            rows = src[block(g, K_PASS), :].rearrange("(p t) k -> p t k", t=PACK)
+            if by_slot:
+                slots = []
+                for t in range(PACK):
+                    raw = keep.tile([P, FEATS], BF16, name="%s_%d" % (name, t))
+                    nc.sync.dma_start(out=raw[:], in_=rows[:, t, :])
+                    slots.append(raw[:].bitcast(F32))
+                return slots
+            raw = keep.tile([P, PACK * FEATS], BF16, name=name)
+            nc.sync.dma_start(out=raw[:], in_=rows.rearrange("p t k -> p (t k)"))
+            words = raw[:].bitcast(F32)
+            return [words[:, block(t, FEATS // 2)] for t in range(PACK)]
+
+        u_raw, e_raw, d_rows, x_rows = {}, {}, {}, {}
+        for c in range(2):
+            u_raw[c] = load_k_first("u_raw%d" % c, user_factors[block(c, K_PASS), :])
+        d_rows[0] = load_items("d0", score_grads, 0, by_slot=True)
+        d_rows[1] = load_items("d1", score_grads, 1, by_slot=SLOT_LOADS > 1)
+        x_rows[0] = load_items("x0", item_feats, 0)
+        for c in range(2):
+            e_raw[0, c] = load_k_first("e_raw0%d" % c, encoder[block(c, K_PASS), block(0, K_PASS)])
+        gain = keep.tile([P, GROUPS, PACK], BF16, name="gain")
+        nc.sync.dma_start(out=gain[:], in_=item_gain.rearrange("(g p t) -> p g t", p=P, t=PACK))
+        d_rows[2] = load_items("d2", score_grads, 2)
+        x_rows[1] = load_items("x1", item_feats, 1)
+        for c in range(2):
+            e_raw[1, c] = load_k_first("e_raw1%d" % c, encoder[block(c, K_PASS), block(1, K_PASS)])
+        d_rows[3] = load_items("d3", score_grads, 3)
+        x_rows[2] = load_items("x2", item_feats, 2)
+        x_rows[3] = load_items("x3", item_feats, 3)
+        step = keep.tile([P, 2, PACK], BF16, name="step")
+        nc.sync.dma_start(out=step[:], in_=step_sizes.rearrange("(h p t) -> p h t", p=P, t=PACK))
+        proj = [load_k_first("proj%d" % h, projection[block(h, K_PASS), :]) for h in range(2)]
+
+        deferred = []
+
+        def run_deferred():
+            for action in deferred:
+                action()
+            deferred.clear()
+
+        def interleave_u(c):
+            staged = stage_tile()
+            nc.vector.tensor_copy(
+                out=staged[:].rearrange("p (n i j) -> p n j i", i=4, j=PACK),
+                in_=u_raw[c][:].rearrange("p j (n i) -> p n j i", i=4),
+            )
+            return staged
+
+        def interleave_e(h, c):
+            staged = stage_tile()
+            copy = nc.scalar.copy if E_ON_SCALAR[h][c] else nc.vector.tensor_copy
+            copy(
+                out=staged[:].rearrange("p (t m i j) -> p m t i j", t=PACK, i=2, j=PACK),
+                in_=e_raw[h, c][:].rearrange("p j (m i t) -> p m t i j", i=2, t=PACK),
+            )
+            return staged
+
+        def transpose_items(slots, name, bufs):
+            pairs = []
+            for pair in range(2):
+                staged = stage_tile()
+                staged_words = staged[:].bitcast(F32)
+                for t in range(2 * pair, 2 * pair + 2):
+                    bank = psum.tile([P, 2, 2, P], F32, name="turn", tag="turn")
+                    for c in range(2):
+                        for u in range(2):
+                            nc.tensor.transpose(bank[:, c, u, :], slots[t][:, 2 * P * c + u : 2 * P * (c + 1) : 2], ident[:])
+                    nc.scalar.copy(
+                        out=staged_words[:, block(t % 2, K_PASS)].rearrange("p (c r u) -> p c r u", c=2, u=2),
+                        in_=bank[:].rearrange("p c u r -> p c r u"),
+                    )
+                mx = mx_tiles(name, bufs=bufs)
+                quantize(mx, staged)
+                run_deferred()
+                pairs.append(mx)
+            return pairs
+
+        def product_bank(items, weights, n):
+            bank = psum.tile([P, PACK, P], F32, name="prod", tag="prod")
+            for t in range(PACK):
+                for c in range(2):
+                    matmul(bank[:, t, :], items[t // 2], block(2 * (t % 2) + c), weights[c], block(n), c == 0, c == 1)
+            return bank
+
+        def interleaved(staged, n):
+            return staged[:, block(n, K_PASS)].rearrange("p (n t) -> p n t", t=PACK)
+
+        g_mx, z_mx = {}, {}
+
+        def item_factor_grads(g, d_mx):
+            staged = stage_tile()
+            for n in range(4):
+                bank = product_bank(d_mx, u_mx, n)
+                nc.scalar.copy(out=interleaved(staged, n), in_=bank[:].rearrange("p t n -> p n t"))
+            g_mx[g] = mx_tiles("g%d" % g)
+            quantize(g_mx[g], staged)
+
+        def encode_chunk(g, x_mx, h, n, staged):
+            bank = product_bank(x_mx, e_mx[h], n)
+            nc.vector.scalar_tensor_tensor(
+                out=interleaved(staged, n),
+                in0=bank[:].rearrange("p t n -> p n t"),
+                scalar=0.0,
+                in1=gain[:, g, :].unsqueeze(1).to_broadcast([P, P, PACK]),
+                op0=ALU.max,
+                op1=ALU.mult,
+            )
+
+        def encode(g, x_mx, h):
+            staged = stage_tile()
+            for n in range(4):
+                encode_chunk(g, x_mx, h, n, staged)
+            z_mx[g, h] = mx_tiles("z%d%d" % (g, h))
+            deferred.append(lambda: quantize(z_mx[g, h], staged))
+
+        u_mx, e_mx = [], {0: [], 1: []}
+        for c in range(2):
+            staged = interleave_u(c)
+            u_mx.append(mx_tiles("u%d" % c))
+            quantize(u_mx[c], staged)
+
+        e_staged = {}
+
+        def quantize_e(h, c):
+            e_mx[h].append(mx_tiles("e%d%d" % (h, c)))
+            quantize(e_mx[h][c], e_staged[h, c])
+
+        d_mx, x_mx = {}, {}
+        neg_step = keep.tile([P, 2, PACK], F32, name="neg_step")
+
+        def negate():
+            nc.vector.tensor_scalar(out=neg_step[:], in0=step[:], scalar1=-1.0, scalar2=None, op0=ALU.mult)
+
+        last = GROUPS - 1
+        y_scales = [keep.tile([P, LATENT], U8, name="y_scales%d" % h, align_bytes=64) for h in range(2)]
+        out_rows = [out_0[block(h, K_PASS), :].rearrange("(p t) l -> p t l", t=PACK) for h in range(2)]
+        out_words = out_1.rearrange("h p l t -> h p (l t)").bitcast(I32)
+        out_scales = out_2.bitcast(I32)
+
+        def encode_last(g, h):
+            staged = stage_tile()
+            z_mx[g, h] = mx_tiles("z%d%d" % (g, h))
+            for n in range(4):
+                encode_chunk(g, x_mx[g], h, n, staged)
+                run_deferred()
+                deferred.append(lambda n=n: quantize(z_mx[g, h], staged, block(n)))
+
+        def step_projection(h, t, cols, acc):
+            for g in range(GROUPS):
+                matmul(acc, z_mx[g, h], block(t), g_mx[g], cols, g == 0, g == last)
+
+        def update(y, h, t, cols, acc):
+            nc.vector.scalar_tensor_tensor(
+                out=y[:, t, :],
+                in0=acc,
+                scalar=neg_step[:, h, t : t + 1],
+                in1=proj[h][:, t, cols],
+                op0=ALU.mult,
+                op1=ALU.add,
+            )
+
+        def stage_planes(y, width, copy):
+            staged = stage_tile()
+            copy(
+                out=staged[:, : PACK * width].rearrange("p (n i t) -> p n t i", i=4, t=PACK),
+                in_=y[:].rearrange("p t (n i) -> p n t i", i=4),
+            )
+            return staged
+
+        def store_planes(h, cols, staged):
+            width = cols.stop - cols.start
+            codes = keep.tile([P, width], U32, name="y_codes%d_%d" % (h, cols.start), align_bytes=64)
+            nc.vector.quantize_mx(out=codes[:].bitcast(FP8X4), scales=y_scales[h][:, cols], in_=staged[:, : PACK * width])
+            nc.sync.dma_start(out=out_words[h, :, cols], in_=codes[:].bitcast(I32))
+
+        def store_scales(h, queues):
+            plane = y_scales[h][:].bitcast(I32)
+            for q in range(4):
+                queues[q % len(queues)].dma_start(out=out_scales[h, 4 * q : 4 * q + 4, :], in_=plane[32 * q : 32 * q + 4, :])
+
+        pieces = []
+        for h in range(2):
+            start = 0
+            for width in TAIL_WIDTHS[h]:
+                pieces.append((h, slice(start, start + width)))
+                start += width
+        waiting = []
+
+        def flush_planes():
+            for h, cols, staged in waiting:
+                store_planes(h, cols, staged)
+                if cols.stop == LATENT:
+                    store_scales(h, [nc.scalar, nc.sync] if h else [nc.sync])
+            waiting.clear()
+
+        def piece(i):
+            h, cols = pieces[i]
+            width = cols.stop - cols.start
+            y = keep.tile([P, PACK, width], F32, name="y%d" % i)
+            tag = TAIL_TAGS[i]
+            for t in range(PACK):
+                acc = psum.tile([P, width], F32, name=tag, tag=tag)
+                step_projection(h, t, cols, acc[:])
+                update(y, h, t, cols, acc[:])
+                run_deferred()
+            nc.sync.dma_start(out=out_rows[h][:, :, cols], in_=y[:])
+            flush_planes()
+            is_last = i == len(pieces) - 1
+            waiting.append((h, cols, stage_planes(y, width, nc.vector.tensor_copy if is_last else nc.scalar.copy)))
+
+        for st in ORDER.split():
+            kind, args = st[0], [int(ch) for ch in st[1:]]
+            if kind == "D":
+                d_mx[args[0]] = transpose_items(d_rows[args[0]], "d", 4)
+            elif kind == "X":
+                x_mx[args[0]] = transpose_items(x_rows[args[0]], "x", 8)
+            elif kind == "G":
+                item_factor_grads(args[0], d_mx[args[0]])
+            elif kind == "A":
+                encode(args[0], x_mx[args[0]], args[1])
+            elif kind == "L":
+                encode_last(args[0], args[1])
+            elif kind == "i":
+                e_staged[args[0], args[1]] = interleave_e(args[0], args[1])
+            elif kind == "q":
+                quantize_e(args[0], args[1])
+            elif kind == "n":
+                negate()
+            elif kind == "f":
+                run_deferred()
+            elif kind == "P":
+                piece(args[0])
+        flush_planes()

@@ -17,38 +17,58 @@ ALU = mybir.AluOpType
 P = 128
 PACK = 4
 K_PASS = P * PACK
+PASSES = FEATS // K_PASS
 GROUPS = ITEMS // K_PASS
-STAGE_BUFS = 7
-TAIL_WIDTHS = ((256, 256), (256, 256))
-E_ON_SCALAR = ((0, 0), (1, 1))
-SLOT_LOADS = 2
-TAIL_TAGS = ("turn", "prod", "turn", "prod", "turn")
-ORDER = "D0 D1 G0 i00 X0 i01 q00 q01 G1 D2 A00 i10 X1 G2 q10 D3 A10 i11 X2 G3 q11 A20 X3 A01 n L30 A11 P0 A21 P1 L31 P2 P3"
+HALVES = HIDDEN // K_PASS
+CHUNKS = K_PASS // P
+ROW_WORDS = FEATS // 2
+PIECE = 256
+
+STAGED_BUFS = 13
+ROWS_BUFS = 4
+K_FIRST_BUFS = 6
+SORTED_BUFS = 8
+D_CODES_BUFS = 4
+
+QUANTISE_PER_RUN = 2
 
 
 def tile_latent_projection_step_h3_kernel(
     tc, item_feats, encoder, item_gain, score_grads, user_factors, projection, step_sizes, out_0, out_1, out_2
 ):
     nc = tc.nc
+    scalar_copy, vector_copy = nc.scalar.copy, nc.vector.tensor_copy
     with ExitStack() as ctx:
-        keep = ctx.enter_context(tc.tile_pool(name="keep", bufs=1))
+        sbuf = ctx.enter_context(tc.tile_pool(name="sbuf", bufs=1))
         psum = ctx.enter_context(tc.psum_pool(name="psum", bufs=4))
         ctx.enter_context(tc.manual_schedule())
 
-        def stage_tile():
-            return keep.tile([P, K_PASS * PACK], BF16, name="stage", tag="stage", bufs=STAGE_BUFS, align_bytes=64)
+        def block(i, width=P):
+            return slice(i * width, (i + 1) * width)
+
+        def staged_tile():
+            return sbuf.tile([P, K_PASS * PACK], BF16, name="staged", tag="staged", bufs=STAGED_BUFS, align_bytes=64)
 
         def mx_tiles(name, bufs=1):
-            codes = keep.tile([P, K_PASS], U32, name=name + "_codes", tag=name + "_codes", bufs=bufs, align_bytes=64)
-            scales = keep.tile([P, K_PASS], U8, name=name + "_scales", tag=name + "_scales", bufs=bufs, align_bytes=64)
+            codes = sbuf.tile([P, K_PASS], U32, name=name + "_codes", tag=name + "_codes", bufs=bufs, align_bytes=64)
+            scales = sbuf.tile([P, K_PASS], U8, name=name + "_scales", tag=name + "_scales", bufs=bufs, align_bytes=64)
             return codes, scales
 
-        def quantize(mx, staged, cols=slice(0, K_PASS), src=None):
-            codes, scales = mx
-            src = src or slice(PACK * cols.start, PACK * cols.stop)
-            nc.vector.quantize_mx(out=codes[:, cols].bitcast(FP8X4), scales=scales[:, cols], in_=staged[:, src])
+        def quantize(mx, staged):
+            nc.vector.quantize_mx(out=mx[0][:].bitcast(FP8X4), scales=mx[1][:], in_=staged[:])
+
+        soon, spare = [], []
+
+        def quantize_entries(entries):
+            for entry in entries:
+                for queue in (soon, spare):
+                    others = [other for other in queue if other is not entry]
+                    queue.clear()
+                    queue.extend(others)
+                quantize(*entry)
 
         def matmul(out, lhs, lhs_cols, rhs, rhs_cols, start, stop):
+            quantize_entries([entry for entry in soon + spare if entry[0] is lhs or entry[0] is rhs])
             nc.tensor.matmul_mx(
                 out=out,
                 lhsT=lhs[0][:, lhs_cols].bitcast(FP8X4),
@@ -59,249 +79,238 @@ def tile_latent_projection_step_h3_kernel(
                 stop=stop,
             )
 
-        def block(i, width=P):
-            return slice(i * width, (i + 1) * width)
-
-        ident = keep.tile([P, P], F32, name="ident")
+        ident = sbuf.tile([P, P], F32, name="ident")
         make_identity(nc, ident[:])
 
-        def load_k_first(name, src):
-            raw = keep.tile([P, PACK, K_PASS], BF16, name=name)
+        def load_k_first(src):
+            raw = sbuf.tile([P, PACK, K_PASS], BF16, name="k_first", tag="k_first", bufs=K_FIRST_BUFS)
             nc.sync.dma_start(out=raw[:], in_=src.rearrange("(p j) n -> p j n", j=PACK))
             return raw
 
-        def load_items(name, src, g, by_slot=False):
+        def load_slots(src, g, first, count, tile_name, bufs=1):
+            raw = sbuf.tile([P, count * FEATS], BF16, name=tile_name, tag=tile_name, bufs=bufs)
             rows = src[block(g, K_PASS), :].rearrange("(p t) k -> p t k", t=PACK)
-            if by_slot:
-                slots = []
-                for t in range(PACK):
-                    raw = keep.tile([P, FEATS], BF16, name="%s_%d" % (name, t))
-                    nc.sync.dma_start(out=raw[:], in_=rows[:, t, :])
-                    slots.append(raw[:].bitcast(F32))
-                return slots
-            raw = keep.tile([P, PACK * FEATS], BF16, name=name)
-            nc.sync.dma_start(out=raw[:], in_=rows.rearrange("p t k -> p (t k)"))
+            nc.sync.dma_start(out=raw[:], in_=rows[:, first : first + count, :].rearrange("p t k -> p (t k)"))
             words = raw[:].bitcast(F32)
-            return [words[:, block(t, FEATS // 2)] for t in range(PACK)]
+            return [words[:, block(t, ROW_WORDS)].rearrange("p (c w u) -> p c u w", c=PASSES, u=2) for t in range(count)]
 
-        u_raw, e_raw, d_rows, x_rows = {}, {}, {}, {}
-        for c in range(2):
-            u_raw[c] = load_k_first("u_raw%d" % c, user_factors[block(c, K_PASS), :])
-        d_rows[0] = load_items("d0", score_grads, 0, by_slot=True)
-        d_rows[1] = load_items("d1", score_grads, 1, by_slot=SLOT_LOADS > 1)
-        x_rows[0] = load_items("x0", item_feats, 0)
-        for c in range(2):
-            e_raw[0, c] = load_k_first("e_raw0%d" % c, encoder[block(c, K_PASS), block(0, K_PASS)])
-        gain = keep.tile([P, GROUPS, PACK], BF16, name="gain")
+        def load_group(src, g):
+            return load_slots(src, g, 0, PACK, "rows", ROWS_BUFS)
+
+        def load_group_in_parts(g, counts):
+            slots = []
+            for count in counts:
+                slots.extend(load_slots(item_feats, g, len(slots), count, "x%d_from%d" % (g, len(slots))))
+            return slots
+
+        def load_encoder(h, c):
+            return load_k_first(encoder[block(c, K_PASS), block(h, K_PASS)])
+
+        e_raw, u_raw, x_words, d_words = {}, {}, {}, {}
+        gain = sbuf.tile([P, GROUPS, PACK], BF16, name="gain")
+        step = sbuf.tile([P, HALVES, PACK], BF16, name="step")
+        e_raw[0, 0] = load_encoder(0, 0)
+        x_words[0] = load_group_in_parts(0, (2, 2))
+        e_raw[0, 1] = load_encoder(0, 1)
+        x_words[1] = load_group_in_parts(1, (1, 1, 1, 1))
         nc.sync.dma_start(out=gain[:], in_=item_gain.rearrange("(g p t) -> p g t", p=P, t=PACK))
-        d_rows[2] = load_items("d2", score_grads, 2)
-        x_rows[1] = load_items("x1", item_feats, 1)
-        for c in range(2):
-            e_raw[1, c] = load_k_first("e_raw1%d" % c, encoder[block(c, K_PASS), block(1, K_PASS)])
-        d_rows[3] = load_items("d3", score_grads, 3)
-        x_rows[2] = load_items("x2", item_feats, 2)
-        x_rows[3] = load_items("x3", item_feats, 3)
-        step = keep.tile([P, 2, PACK], BF16, name="step")
-        nc.sync.dma_start(out=step[:], in_=step_sizes.rearrange("(h p t) -> p h t", p=P, t=PACK))
-        proj = [load_k_first("proj%d" % h, projection[block(h, K_PASS), :]) for h in range(2)]
+        for c in range(PASSES):
+            e_raw[1, c] = load_encoder(1, c)
+        d_words[0] = load_group(score_grads, 0)
+        for c in range(PASSES):
+            u_raw[c] = load_k_first(user_factors[block(c, K_PASS), :])
+        x_words[2] = load_group(item_feats, 2)
+        x_words[3] = load_group(item_feats, 3)
+        d_words[1] = load_group(score_grads, 1)
 
-        deferred = []
+        e_mx, u_mx = [{}, {}], {}
+        x_mx, d_mx, z_mx, g_mx = {}, {}, {}, {}
 
-        def run_deferred():
-            for action in deferred:
-                action()
-            deferred.clear()
-
-        def interleave_u(c):
-            staged = stage_tile()
-            nc.vector.tensor_copy(
-                out=staged[:].rearrange("p (n i j) -> p n j i", i=4, j=PACK),
-                in_=u_raw[c][:].rearrange("p j (n i) -> p n j i", i=4),
-            )
-            return staged
-
-        def interleave_e(h, c):
-            staged = stage_tile()
-            copy = nc.scalar.copy if E_ON_SCALAR[h][c] else nc.vector.tensor_copy
+        def stage_encoder(h, c, copy):
+            staged = staged_tile()
             copy(
                 out=staged[:].rearrange("p (t m i j) -> p m t i j", t=PACK, i=2, j=PACK),
                 in_=e_raw[h, c][:].rearrange("p j (m i t) -> p m t i j", i=2, t=PACK),
             )
-            return staged
+            e_mx[h][c] = mx_tiles("e%d%d" % (h, c))
+            return e_mx[h][c], staged
 
-        def transpose_items(slots, name, bufs):
+        def interleave(copy, staged, rows):
+            copy(
+                out=staged.rearrange("p (n i j) -> p n j i", i=4, j=PACK),
+                in_=rows.rearrange("p j (n i) -> p n j i", i=4),
+            )
+
+        def stage_user_factors(c):
+            staged = staged_tile()
+            interleave(scalar_copy, staged[:], u_raw[c][:])
+            u_mx[c] = mx_tiles("u%d" % c)
+            return u_mx[c], staged
+
+        def sort_words(slots, pair, copy):
+            for t in (2 * pair, 2 * pair + 1):
+                ordered = sbuf.tile([P, PASSES, 2, P], F32, name="sorted", tag="sorted", bufs=SORTED_BUFS)
+                copy(
+                    out=ordered[:].rearrange("p c u (b i) -> p c b u i", i=4),
+                    in_=slots[t].rearrange("p c u (b i) -> p c b u i", i=4),
+                )
+                slots[t] = ordered
+
+        def turn_items(slots, name, bufs):
             pairs = []
             for pair in range(2):
-                staged = stage_tile()
-                staged_words = staged[:].bitcast(F32)
-                for t in range(2 * pair, 2 * pair + 2):
-                    bank = psum.tile([P, 2, 2, P], F32, name="turn", tag="turn")
-                    for c in range(2):
+                staged = staged_tile()
+                for t in range(2):
+                    bank = psum.tile([P, PASSES, 2, P], F32, name="turn", tag="turn")
+                    for c in range(PASSES):
                         for u in range(2):
-                            nc.tensor.transpose(bank[:, c, u, :], slots[t][:, 2 * P * c + u : 2 * P * (c + 1) : 2], ident[:])
-                    nc.scalar.copy(
-                        out=staged_words[:, block(t % 2, K_PASS)].rearrange("p (c r u) -> p c r u", c=2, u=2),
+                            nc.tensor.transpose(bank[:, c, u, :], slots[2 * pair + t][:, c, u, :], ident[:])
+                    scalar_copy(
+                        out=staged[:].bitcast(F32)[:, block(t, K_PASS)].rearrange("p (c r u) -> p c r u", c=PASSES, u=2),
                         in_=bank[:].rearrange("p c u r -> p c r u"),
                     )
-                mx = mx_tiles(name, bufs=bufs)
-                quantize(mx, staged)
-                run_deferred()
+                mx = mx_tiles(name, bufs)
+                if pair == 0:
+                    quantize_entries((soon + spare[:-1])[:QUANTISE_PER_RUN])
+                    quantize(mx, staged)
+                else:
+                    soon.append((mx, staged))
                 pairs.append(mx)
             return pairs
+
+        def turn_x(g):
+            x_mx[g] = turn_items(x_words[g], "x", 2 * GROUPS)
+
+        def turn_d(g):
+            d_mx[g] = turn_items(d_words[g], "d", D_CODES_BUFS)
 
         def product_bank(items, weights, n):
             bank = psum.tile([P, PACK, P], F32, name="prod", tag="prod")
             for t in range(PACK):
-                for c in range(2):
-                    matmul(bank[:, t, :], items[t // 2], block(2 * (t % 2) + c), weights[c], block(n), c == 0, c == 1)
-            return bank
+                for c in range(PASSES):
+                    lhs_cols = block(PASSES * (t % 2) + c)
+                    matmul(bank[:, t, :], items[t // 2], lhs_cols, weights[c], block(n), c == 0, c == PASSES - 1)
+            return bank[:].rearrange("p t n -> p n t")
 
-        def interleaved(staged, n):
+        def staged_chunk(staged, n):
             return staged[:, block(n, K_PASS)].rearrange("p (n t) -> p n t", t=PACK)
 
-        g_mx, z_mx = {}, {}
-
-        def item_factor_grads(g, d_mx):
-            staged = stage_tile()
-            for n in range(4):
-                bank = product_bank(d_mx, u_mx, n)
-                nc.scalar.copy(out=interleaved(staged, n), in_=bank[:].rearrange("p t n -> p n t"))
-            g_mx[g] = mx_tiles("g%d" % g)
-            quantize(g_mx[g], staged)
-
-        def encode_chunk(g, x_mx, h, n, staged):
-            bank = product_bank(x_mx, e_mx[h], n)
-            nc.vector.scalar_tensor_tensor(
-                out=interleaved(staged, n),
-                in0=bank[:].rearrange("p t n -> p n t"),
-                scalar=0.0,
-                in1=gain[:, g, :].unsqueeze(1).to_broadcast([P, P, PACK]),
-                op0=ALU.max,
-                op1=ALU.mult,
-            )
-
-        def encode(g, x_mx, h):
-            staged = stage_tile()
-            for n in range(4):
-                encode_chunk(g, x_mx, h, n, staged)
+        def encode(g, h):
+            staged = staged_tile()
+            for n in range(CHUNKS):
+                nc.vector.scalar_tensor_tensor(
+                    out=staged_chunk(staged, n),
+                    in0=product_bank(x_mx[g], e_mx[h], n),
+                    scalar=0.0,
+                    in1=gain[:, g, :].unsqueeze(1).to_broadcast([P, P, PACK]),
+                    op0=ALU.max,
+                    op1=ALU.mult,
+                )
+                if n > 0:
+                    quantize_entries(soon[:1])
             z_mx[g, h] = mx_tiles("z%d%d" % (g, h))
-            deferred.append(lambda: quantize(z_mx[g, h], staged))
+            spare.append((z_mx[g, h], staged))
 
-        u_mx, e_mx = [], {0: [], 1: []}
-        for c in range(2):
-            staged = interleave_u(c)
-            u_mx.append(mx_tiles("u%d" % c))
-            quantize(u_mx[c], staged)
+        def factor_grads(g):
+            quantize_entries(soon + spare)
+            staged = staged_tile()
+            for n in range(CHUNKS):
+                scalar_copy(out=staged_chunk(staged, n), in_=product_bank(d_mx[g], u_mx, n))
+            g_mx[g] = mx_tiles("g%d" % g)
+            spare.append((g_mx[g], staged))
 
-        e_staged = {}
+        quantize(*stage_encoder(0, 0, vector_copy))
+        turn_x(0)
+        soon.append(stage_encoder(0, 1, vector_copy))
+        quantize_entries(soon[:])
+        turn_x(1)
+        encode(0, 0)
+        soon.append(stage_encoder(1, 0, scalar_copy))
+        e_last = stage_encoder(1, 1, scalar_copy)
+        encode(1, 0)
+        soon.append(e_last)
+        turn_d(0)
+        d_words[2] = load_group(score_grads, 2)
+        u_first = stage_user_factors(0)
+        encode(0, 1)
+        soon.append(u_first)
+        turn_x(2)
+        d_words[3] = load_group(score_grads, 3)
+        nc.sync.dma_start(out=step[:], in_=step_sizes.rearrange("(h p t) -> p h t", p=P, t=PACK))
+        proj = [load_k_first(projection[block(h, K_PASS), :]) for h in range(HALVES)]
+        soon.append(stage_user_factors(1))
+        encode(1, 1)
+        for pair in range(2):
+            sort_words(x_words[3], pair, scalar_copy)
+        encode(2, 0)
+        factor_grads(0)
+        for pair in range(2):
+            sort_words(d_words[1], pair, vector_copy)
+        turn_x(3)
+        sort_words(d_words[2], 0, scalar_copy)
+        encode(2, 1)
+        turn_d(1)
+        sort_words(d_words[2], 1, scalar_copy)
+        encode(3, 0)
+        turn_d(2)
+        for pair in range(2):
+            sort_words(d_words[3], pair, vector_copy)
+        factor_grads(1)
+        turn_d(3)
+        factor_grads(2)
+        encode(3, 1)
+        neg_step = sbuf.tile([P, HALVES, PACK], F32, name="neg_step")
+        nc.vector.tensor_scalar(out=neg_step[:], in0=step[:], scalar1=-1.0, scalar2=None, op0=ALU.mult)
+        factor_grads(3)
 
-        def quantize_e(h, c):
-            e_mx[h].append(mx_tiles("e%d%d" % (h, c)))
-            quantize(e_mx[h][c], e_staged[h, c])
-
-        d_mx, x_mx = {}, {}
-        neg_step = keep.tile([P, 2, PACK], F32, name="neg_step")
-
-        def negate():
-            nc.vector.tensor_scalar(out=neg_step[:], in0=step[:], scalar1=-1.0, scalar2=None, op0=ALU.mult)
-
-        last = GROUPS - 1
-        y_scales = [keep.tile([P, LATENT], U8, name="y_scales%d" % h, align_bytes=64) for h in range(2)]
-        out_rows = [out_0[block(h, K_PASS), :].rearrange("(p t) l -> p t l", t=PACK) for h in range(2)]
         out_words = out_1.rearrange("h p l t -> h p (l t)").bitcast(I32)
         out_scales = out_2.bitcast(I32)
+        y_scales = [sbuf.tile([P, LATENT], U8, name="y_scales%d" % h, align_bytes=64) for h in range(HALVES)]
+        pieces = [(h, block(i, PIECE)) for h in range(HALVES) for i in range(LATENT // PIECE)]
+        last_piece = len(pieces) - 1
 
-        def encode_last(g, h):
-            staged = stage_tile()
-            z_mx[g, h] = mx_tiles("z%d%d" % (g, h))
-            for n in range(4):
-                encode_chunk(g, x_mx[g], h, n, staged)
-                run_deferred()
-                deferred.append(lambda n=n: quantize(z_mx[g, h], staged, block(n)))
-
-        def step_projection(h, t, cols, acc):
-            for g in range(GROUPS):
-                matmul(acc, z_mx[g, h], block(t), g_mx[g], cols, g == 0, g == last)
-
-        def update(y, h, t, cols, acc):
-            nc.vector.scalar_tensor_tensor(
-                out=y[:, t, :],
-                in0=acc,
-                scalar=neg_step[:, h, t : t + 1],
-                in1=proj[h][:, t, cols],
-                op0=ALU.mult,
-                op1=ALU.add,
-            )
-
-        def stage_planes(y, width, copy):
-            staged = stage_tile()
-            copy(
-                out=staged[:, : PACK * width].rearrange("p (n i t) -> p n t i", i=4, t=PACK),
-                in_=y[:].rearrange("p t (n i) -> p n t i", i=4),
-            )
-            return staged
-
-        def store_planes(h, cols, staged):
-            width = cols.stop - cols.start
-            codes = keep.tile([P, width], U32, name="y_codes%d_%d" % (h, cols.start), align_bytes=64)
-            nc.vector.quantize_mx(out=codes[:].bitcast(FP8X4), scales=y_scales[h][:, cols], in_=staged[:, : PACK * width])
-            nc.sync.dma_start(out=out_words[h, :, cols], in_=codes[:].bitcast(I32))
-
-        def store_scales(h, queues):
-            plane = y_scales[h][:].bitcast(I32)
-            for q in range(4):
-                queues[q % len(queues)].dma_start(out=out_scales[h, 4 * q : 4 * q + 4, :], in_=plane[32 * q : 32 * q + 4, :])
-
-        pieces = []
-        for h in range(2):
-            start = 0
-            for width in TAIL_WIDTHS[h]:
-                pieces.append((h, slice(start, start + width)))
-                start += width
-        waiting = []
-
-        def flush_planes():
-            for h, cols, staged in waiting:
-                store_planes(h, cols, staged)
-                if cols.stop == LATENT:
-                    store_scales(h, [nc.scalar, nc.sync] if h else [nc.sync])
-            waiting.clear()
-
-        def piece(i):
+        def store_planes(i, staged):
             h, cols = pieces[i]
-            width = cols.stop - cols.start
-            y = keep.tile([P, PACK, width], F32, name="y%d" % i)
-            tag = TAIL_TAGS[i]
-            for t in range(PACK):
-                acc = psum.tile([P, width], F32, name=tag, tag=tag)
-                step_projection(h, t, cols, acc[:])
-                update(y, h, t, cols, acc[:])
-                run_deferred()
-            nc.sync.dma_start(out=out_rows[h][:, :, cols], in_=y[:])
-            flush_planes()
-            is_last = i == len(pieces) - 1
-            waiting.append((h, cols, stage_planes(y, width, nc.vector.tensor_copy if is_last else nc.scalar.copy)))
+            codes = sbuf.tile([P, PIECE], U32, name="y_codes%d" % i, align_bytes=64)
+            nc.vector.quantize_mx(out=codes[:].bitcast(FP8X4), scales=y_scales[h][:, cols], in_=staged[:, : PACK * PIECE])
+            nc.sync.dma_start(out=out_words[h, :, cols], in_=codes[:].bitcast(I32))
+            if cols.stop == LATENT:
+                for q in range(4):
+                    queue = nc.scalar if i == last_piece and q % 2 == 0 else nc.sync
+                    queue.dma_start(out=out_scales[h, block(q, 4), :], in_=y_scales[h][:].bitcast(I32)[32 * q : 32 * q + 4, :])
 
-        for st in ORDER.split():
-            kind, args = st[0], [int(ch) for ch in st[1:]]
-            if kind == "D":
-                d_mx[args[0]] = transpose_items(d_rows[args[0]], "d", 4)
-            elif kind == "X":
-                x_mx[args[0]] = transpose_items(x_rows[args[0]], "x", 8)
-            elif kind == "G":
-                item_factor_grads(args[0], d_mx[args[0]])
-            elif kind == "A":
-                encode(args[0], x_mx[args[0]], args[1])
-            elif kind == "L":
-                encode_last(args[0], args[1])
-            elif kind == "i":
-                e_staged[args[0], args[1]] = interleave_e(args[0], args[1])
-            elif kind == "q":
-                quantize_e(args[0], args[1])
-            elif kind == "n":
-                negate()
-            elif kind == "f":
-                run_deferred()
-            elif kind == "P":
-                piece(args[0])
-        flush_planes()
+        y_staged = None
+        for i, (h, cols) in enumerate(pieces):
+            y = sbuf.tile([P, PACK, PIECE], F32, name="y%d" % i)
+            out_rows = out_0[block(h, K_PASS), cols].rearrange("(p t) l -> p t l", t=PACK)
+            banks = "turn" if i % 2 == 0 else "prod"
+            sums = [psum.tile([P, PIECE], F32, name=banks, tag=banks) for t in range(PACK)]
+
+            def grad_pass(t, g):
+                matmul(sums[t][:], z_mx[g, h], block(t), g_mx[g], cols, g == 0, g == GROUPS - 1)
+
+            early = GROUPS - 1 if i == 0 else 0
+            for g in range(early):
+                for t in range(PACK):
+                    grad_pass(t, g)
+            for t in range(PACK):
+                for g in range(early, GROUPS):
+                    grad_pass(t, g)
+                nc.vector.scalar_tensor_tensor(
+                    out=y[:, t, :],
+                    in0=sums[t][:],
+                    scalar=neg_step[:, h, t : t + 1],
+                    in1=proj[h][:, t, cols],
+                    op0=ALU.mult,
+                    op1=ALU.add,
+                )
+                if i > 0 and t == (PACK - 1 if i == last_piece else PACK - 2):
+                    store_planes(i - 1, y_staged)
+                if t % 2 == 1:
+                    nc.sync.dma_start(out=out_rows[:, t - 1 : t + 1, :], in_=y[:, t - 1 : t + 1, :])
+            y_staged = staged_tile()
+            on_vector = PIECE // 2 if i == last_piece else 0
+            interleave(scalar_copy, y_staged[:, PACK * on_vector : PACK * PIECE], y[:, :, on_vector:])
+            if on_vector:
+                interleave(vector_copy, y_staged[:, : PACK * on_vector], y[:, :, :on_vector])
+        store_planes(last_piece, y_staged)

from contextlib import ExitStack

import concourse.mybir as mybir
from concourse.masks import make_identity

ITEMS, FEATS, USERS, HIDDEN, LATENT = 2048, 1024, 1024, 1024, 512
FLOPS = 2 * ITEMS * (FEATS * HIDDEN + USERS * LATENT + HIDDEN * LATENT)

F32 = mybir.dt.float32
BF16 = mybir.dt.bfloat16
I32 = mybir.dt.int32
U32 = mybir.dt.uint32
U8 = mybir.dt.uint8
FP8X4 = mybir.dt.float8_e4m3fn_x4
ALU = mybir.AluOpType

P = 128
PACK = 4
K_PASS = P * PACK
PASSES = FEATS // K_PASS
GROUPS = ITEMS // K_PASS
HALVES = HIDDEN // K_PASS
CHUNKS = K_PASS // P
ROW_WORDS = FEATS // 2
PIECE = 256

STAGED_BUFS = 13
ROWS_BUFS = 4
K_FIRST_BUFS = 6
SORTED_BUFS = 8
D_CODES_BUFS = 4

QUANTISE_PER_RUN = 2


def tile_latent_projection_step_h3_kernel(
    tc, item_feats, encoder, item_gain, score_grads, user_factors, projection, step_sizes, out_0, out_1, out_2
):
    nc = tc.nc
    scalar_copy, vector_copy = nc.scalar.copy, nc.vector.tensor_copy
    with ExitStack() as ctx:
        sbuf = ctx.enter_context(tc.tile_pool(name="sbuf", bufs=1))
        psum = ctx.enter_context(tc.psum_pool(name="psum", bufs=4))
        ctx.enter_context(tc.manual_schedule())

        def block(i, width=P):
            return slice(i * width, (i + 1) * width)

        def staged_tile():
            return sbuf.tile([P, K_PASS * PACK], BF16, name="staged", tag="staged", bufs=STAGED_BUFS, align_bytes=64)

        def mx_tiles(name, bufs=1):
            codes = sbuf.tile([P, K_PASS], U32, name=name + "_codes", tag=name + "_codes", bufs=bufs, align_bytes=64)
            scales = sbuf.tile([P, K_PASS], U8, name=name + "_scales", tag=name + "_scales", bufs=bufs, align_bytes=64)
            return codes, scales

        def quantize(mx, staged):
            nc.vector.quantize_mx(out=mx[0][:].bitcast(FP8X4), scales=mx[1][:], in_=staged[:])

        soon, spare = [], []

        def quantize_entries(entries):
            for entry in entries:
                for queue in (soon, spare):
                    others = [other for other in queue if other is not entry]
                    queue.clear()
                    queue.extend(others)
                quantize(*entry)

        def matmul(out, lhs, lhs_cols, rhs, rhs_cols, start, stop):
            quantize_entries([entry for entry in soon + spare if entry[0] is lhs or entry[0] is rhs])
            nc.tensor.matmul_mx(
                out=out,
                lhsT=lhs[0][:, lhs_cols].bitcast(FP8X4),
                lhsT_scale=lhs[1][:, lhs_cols],
                rhs=rhs[0][:, rhs_cols].bitcast(FP8X4),
                rhs_scale=rhs[1][:, rhs_cols],
                start=start,
                stop=stop,
            )

        ident = sbuf.tile([P, P], F32, name="ident")
        make_identity(nc, ident[:])

        def load_k_first(src):
            raw = sbuf.tile([P, PACK, K_PASS], BF16, name="k_first", tag="k_first", bufs=K_FIRST_BUFS)
            nc.sync.dma_start(out=raw[:], in_=src.rearrange("(p j) n -> p j n", j=PACK))
            return raw

        def load_slots(src, g, first, count, tile_name, bufs=1):
            raw = sbuf.tile([P, count * FEATS], BF16, name=tile_name, tag=tile_name, bufs=bufs)
            rows = src[block(g, K_PASS), :].rearrange("(p t) k -> p t k", t=PACK)
            nc.sync.dma_start(out=raw[:], in_=rows[:, first : first + count, :].rearrange("p t k -> p (t k)"))
            words = raw[:].bitcast(F32)
            return [words[:, block(t, ROW_WORDS)].rearrange("p (c w u) -> p c u w", c=PASSES, u=2) for t in range(count)]

        def load_group(src, g):
            return load_slots(src, g, 0, PACK, "rows", ROWS_BUFS)

        def load_group_in_parts(g, counts):
            slots = []
            for count in counts:
                slots.extend(load_slots(item_feats, g, len(slots), count, "x%d_from%d" % (g, len(slots))))
            return slots

        def load_encoder(h, c):
            return load_k_first(encoder[block(c, K_PASS), block(h, K_PASS)])

        e_raw, u_raw, x_words, d_words = {}, {}, {}, {}
        gain = sbuf.tile([P, GROUPS, PACK], BF16, name="gain")
        step = sbuf.tile([P, HALVES, PACK], BF16, name="step")
        e_raw[0, 0] = load_encoder(0, 0)
        x_words[0] = load_group_in_parts(0, (2, 2))
        e_raw[0, 1] = load_encoder(0, 1)
        x_words[1] = load_group_in_parts(1, (1, 1, 1, 1))
        nc.sync.dma_start(out=gain[:], in_=item_gain.rearrange("(g p t) -> p g t", p=P, t=PACK))
        for c in range(PASSES):
            e_raw[1, c] = load_encoder(1, c)
        d_words[0] = load_group(score_grads, 0)
        for c in range(PASSES):
            u_raw[c] = load_k_first(user_factors[block(c, K_PASS), :])
        x_words[2] = load_group(item_feats, 2)
        x_words[3] = load_group(item_feats, 3)
        d_words[1] = load_group(score_grads, 1)

        e_mx, u_mx = [{}, {}], {}
        x_mx, d_mx, z_mx, g_mx = {}, {}, {}, {}

        def stage_encoder(h, c, copy):
            staged = staged_tile()
            copy(
                out=staged[:].rearrange("p (t m i j) -> p m t i j", t=PACK, i=2, j=PACK),
                in_=e_raw[h, c][:].rearrange("p j (m i t) -> p m t i j", i=2, t=PACK),
            )
            e_mx[h][c] = mx_tiles("e%d%d" % (h, c))
            return e_mx[h][c], staged

        def interleave(copy, staged, rows):
            copy(
                out=staged.rearrange("p (n i j) -> p n j i", i=4, j=PACK),
                in_=rows.rearrange("p j (n i) -> p n j i", i=4),
            )

        def stage_user_factors(c):
            staged = staged_tile()
            interleave(scalar_copy, staged[:], u_raw[c][:])
            u_mx[c] = mx_tiles("u%d" % c)
            return u_mx[c], staged

        def sort_words(slots, pair, copy):
            for t in (2 * pair, 2 * pair + 1):
                ordered = sbuf.tile([P, PASSES, 2, P], F32, name="sorted", tag="sorted", bufs=SORTED_BUFS)
                copy(
                    out=ordered[:].rearrange("p c u (b i) -> p c b u i", i=4),
                    in_=slots[t].rearrange("p c u (b i) -> p c b u i", i=4),
                )
                slots[t] = ordered

        def turn_items(slots, name, bufs):
            pairs = []
            for pair in range(2):
                staged = staged_tile()
                for t in range(2):
                    bank = psum.tile([P, PASSES, 2, P], F32, name="turn", tag="turn")
                    for c in range(PASSES):
                        for u in range(2):
                            nc.tensor.transpose(bank[:, c, u, :], slots[2 * pair + t][:, c, u, :], ident[:])
                    scalar_copy(
                        out=staged[:].bitcast(F32)[:, block(t, K_PASS)].rearrange("p (c r u) -> p c r u", c=PASSES, u=2),
                        in_=bank[:].rearrange("p c u r -> p c r u"),
                    )
                mx = mx_tiles(name, bufs)
                if pair == 0:
                    quantize_entries((soon + spare[:-1])[:QUANTISE_PER_RUN])
                    quantize(mx, staged)
                else:
                    soon.append((mx, staged))
                pairs.append(mx)
            return pairs

        def turn_x(g):
            x_mx[g] = turn_items(x_words[g], "x", 2 * GROUPS)

        def turn_d(g):
            d_mx[g] = turn_items(d_words[g], "d", D_CODES_BUFS)

        def product_bank(items, weights, n):
            bank = psum.tile([P, PACK, P], F32, name="prod", tag="prod")
            for t in range(PACK):
                for c in range(PASSES):
                    lhs_cols = block(PASSES * (t % 2) + c)
                    matmul(bank[:, t, :], items[t // 2], lhs_cols, weights[c], block(n), c == 0, c == PASSES - 1)
            return bank[:].rearrange("p t n -> p n t")

        def staged_chunk(staged, n):
            return staged[:, block(n, K_PASS)].rearrange("p (n t) -> p n t", t=PACK)

        def encode(g, h):
            staged = staged_tile()
            for n in range(CHUNKS):
                nc.vector.scalar_tensor_tensor(
                    out=staged_chunk(staged, n),
                    in0=product_bank(x_mx[g], e_mx[h], n),
                    scalar=0.0,
                    in1=gain[:, g, :].unsqueeze(1).to_broadcast([P, P, PACK]),
                    op0=ALU.max,
                    op1=ALU.mult,
                )
                if n > 0:
                    quantize_entries(soon[:1])
            z_mx[g, h] = mx_tiles("z%d%d" % (g, h))
            spare.append((z_mx[g, h], staged))

        def factor_grads(g):
            quantize_entries(soon + spare)
            staged = staged_tile()
            for n in range(CHUNKS):
                scalar_copy(out=staged_chunk(staged, n), in_=product_bank(d_mx[g], u_mx, n))
            g_mx[g] = mx_tiles("g%d" % g)
            spare.append((g_mx[g], staged))

        quantize(*stage_encoder(0, 0, vector_copy))
        turn_x(0)
        soon.append(stage_encoder(0, 1, vector_copy))
        quantize_entries(soon[:])
        turn_x(1)
        encode(0, 0)
        soon.append(stage_encoder(1, 0, scalar_copy))
        e_last = stage_encoder(1, 1, scalar_copy)
        encode(1, 0)
        soon.append(e_last)
        turn_d(0)
        d_words[2] = load_group(score_grads, 2)
        u_first = stage_user_factors(0)
        encode(0, 1)
        soon.append(u_first)
        turn_x(2)
        d_words[3] = load_group(score_grads, 3)
        nc.sync.dma_start(out=step[:], in_=step_sizes.rearrange("(h p t) -> p h t", p=P, t=PACK))
        proj = [load_k_first(projection[block(h, K_PASS), :]) for h in range(HALVES)]
        soon.append(stage_user_factors(1))
        encode(1, 1)
        for pair in range(2):
            sort_words(x_words[3], pair, scalar_copy)
        encode(2, 0)
        factor_grads(0)
        for pair in range(2):
            sort_words(d_words[1], pair, vector_copy)
        turn_x(3)
        sort_words(d_words[2], 0, scalar_copy)
        encode(2, 1)
        turn_d(1)
        sort_words(d_words[2], 1, scalar_copy)
        encode(3, 0)
        turn_d(2)
        for pair in range(2):
            sort_words(d_words[3], pair, vector_copy)
        factor_grads(1)
        turn_d(3)
        factor_grads(2)
        encode(3, 1)
        neg_step = sbuf.tile([P, HALVES, PACK], F32, name="neg_step")
        nc.vector.tensor_scalar(out=neg_step[:], in0=step[:], scalar1=-1.0, scalar2=None, op0=ALU.mult)
        factor_grads(3)

        out_words = out_1.rearrange("h p l t -> h p (l t)").bitcast(I32)
        out_scales = out_2.bitcast(I32)
        y_scales = [sbuf.tile([P, LATENT], U8, name="y_scales%d" % h, align_bytes=64) for h in range(HALVES)]
        pieces = [(h, block(i, PIECE)) for h in range(HALVES) for i in range(LATENT // PIECE)]
        last_piece = len(pieces) - 1

        def store_planes(i, staged):
            h, cols = pieces[i]
            codes = sbuf.tile([P, PIECE], U32, name="y_codes%d" % i, align_bytes=64)
            nc.vector.quantize_mx(out=codes[:].bitcast(FP8X4), scales=y_scales[h][:, cols], in_=staged[:, : PACK * PIECE])
            nc.sync.dma_start(out=out_words[h, :, cols], in_=codes[:].bitcast(I32))
            if cols.stop == LATENT:
                for q in range(4):
                    queue = nc.scalar if i == last_piece and q % 2 == 0 else nc.sync
                    queue.dma_start(out=out_scales[h, block(q, 4), :], in_=y_scales[h][:].bitcast(I32)[32 * q : 32 * q + 4, :])

        y_staged = None
        for i, (h, cols) in enumerate(pieces):
            y = sbuf.tile([P, PACK, PIECE], F32, name="y%d" % i)
            out_rows = out_0[block(h, K_PASS), cols].rearrange("(p t) l -> p t l", t=PACK)
            banks = "turn" if i % 2 == 0 else "prod"
            sums = [psum.tile([P, PIECE], F32, name=banks, tag=banks) for t in range(PACK)]

            def grad_pass(t, g):
                matmul(sums[t][:], z_mx[g, h], block(t), g_mx[g], cols, g == 0, g == GROUPS - 1)

            early = GROUPS - 1 if i == 0 else 0
            for g in range(early):
                for t in range(PACK):
                    grad_pass(t, g)
            for t in range(PACK):
                for g in range(early, GROUPS):
                    grad_pass(t, g)
                nc.vector.scalar_tensor_tensor(
                    out=y[:, t, :],
                    in0=sums[t][:],
                    scalar=neg_step[:, h, t : t + 1],
                    in1=proj[h][:, t, cols],
                    op0=ALU.mult,
                    op1=ALU.add,
                )
                if i > 0 and t == (PACK - 1 if i == last_piece else PACK - 2):
                    store_planes(i - 1, y_staged)
                if t % 2 == 1:
                    nc.sync.dma_start(out=out_rows[:, t - 1 : t + 1, :], in_=y[:, t - 1 : t + 1, :])
            y_staged = staged_tile()
            on_vector = PIECE // 2 if i == last_piece else 0
            interleave(scalar_copy, y_staged[:, PACK * on_vector : PACK * PIECE], y[:, :, on_vector:])
            if on_vector:
                interleave(vector_copy, y_staged[:, : PACK * on_vector], y[:, :, :on_vector])
        store_planes(last_piece, y_staged)
